import numpy as np, ml_dtypes
CORES = [12,28,44,60,3,19,35,51]
N = 8
GR, GC, HH, WW = 4, 2, 4, 64
def setup_inputs(rng):
    return {"x": rng.standard_normal((N, 128, HH * WW), dtype=np.float32).astype(ml_dtypes.bfloat16), "w": rng.standard_normal((N, 128, 9 * 128), dtype=np.float32).astype(ml_dtypes.bfloat16)}
def setup_inputs_big(rng):
    d = setup_inputs(rng)
    for k in ("x", "w"): d[k] = (d[k].astype(np.float32) * 1024.0).astype(d[k].dtype)
    return d
def setup_inputs_small(rng):
    d = setup_inputs(rng)
    for k in ("x", "w"): d[k] = (d[k].astype(np.float32) * (1 / 1024.0)).astype(d[k].dtype)
    return d
def setup_inputs_apart(rng):
    d = setup_inputs(rng)
    f = (10.0 ** rng.permutation(np.linspace(-1.5, 1.5, N))).astype(np.float32).reshape(N, 1, 1)
    for k in ("x", "w"): d[k] = (d[k].astype(np.float32) * f).astype(d[k].dtype)
    return d
def reference(x, w):
    X = x.astype(np.float64).reshape(GR, GC, 128, HH, WW); W = w.astype(np.float64)
    g = np.concatenate([np.concatenate(list(X[i]), axis=2) for i in range(GR)], axis=1)
    y = np.zeros((N, 128, HH * WW))
    for r in range(N):
        i0, j0 = HH * (r // GC), WW * (r % GC)
        for a in range(3):
            for b in range(3):
                sh = np.roll(g, (-2 * (a - 1), -2 * (b - 1)), axis=(1, 2))[:, i0:i0 + HH, j0:j0 + WW]
                y[r] += W[r][:, 128 * (3 * a + b):128 * (3 * a + b) + 128].T @ sh.reshape(128, HH * WW)
    return {"y": y.astype(ml_dtypes.bfloat16 if x.dtype != np.float64 else np.float64)}

from concourse.bass import DstId, RemoteDMATransfer

GR, GC, HH, WW = 4, 2, 4, 64
K_RANK = 8
K_RELAY = 8

SCRATCH = {
    "X": ("sbuf", [128, 4, 64], "bfloat16"),
    "W": ("sbuf", [128, 1152], "bfloat16"),
    "U": ("sbuf", [128, 2, 64], "bfloat16"),
    "D": ("sbuf", [128, 2, 64], "bfloat16"),
    "EP": ("sbuf", [128, 4, 4], "bfloat16"),
    "EH": ("sbuf", [128, 4, 4], "bfloat16"),
    "EU": ("sbuf", [128, 4, 4], "bfloat16"),
    "ED": ("sbuf", [128, 4, 4], "bfloat16"),
    "Y0": ("sbuf", [128, 2, 64], "bfloat16"),
    "Y1": ("sbuf", [128, 2, 64], "bfloat16"),
    "P0": ("psum", [128, 8, 64], "float32"),
    "P1": ("psum", [128, 8, 64], "float32"),
}
SEMAPHORES = ["xa", "xb", "wl", "pk", "su", "sd", "se", "sel", "sent", "mm0", "mm1", "ev0", "ev1", "st0", "st1"]


def _rank(R, C):
    return (R % GR) * GC + (C % GC)


def _bits(mask):
    return [e for e in range(mask.bit_length()) if (mask >> e) & 1]


def _pick(mask, k):
    b = _bits(mask)
    return b[::len(b) // k][:k]


def _m(engines):
    return sum(1 << e for e in engines)


def _plan(T, topo):
    calls, inc, key = {}, {}, {}
    full = (0, 4)

    def add(core, waits, transfers, k):
        calls.setdefault(core, []).append((waits, transfers))
        for t in transfers:
            n = len(_bits(t["mask"]))
            for (d, _b, _s) in t["dsts"]:
                inc[(d, t["sem"])] = inc.get((d, t["sem"]), 0) + n
                key[(d, t["sem"])] = max(key.get((d, t["sem"]), 0), k)
            inc[(core, "sent")] = inc.get((core, "sent"), 0) + n

    relay_jobs = []
    for r, c in enumerate(T.cores):
        R, C = divmod(r, GC)
        cr = T.cores
        rows = [(cr[_rank(R - 1, C)], (0, 2), "D", "sd", "xa"), (cr[_rank(R + 1, C)], (2, 4), "U", "su", "xb")]
        edges = [(cr[_rank(R, C + 1)], "EH", full), (cr[_rank(R - 1, C + 1)], "ED", (0, 2)), (cr[_rank(R + 1, C + 1)], "EU", (2, 4))]
        far = [d for (d, *_x) in rows + edges if not topo.may_write(c, d)]
        free = [h for h in range(topo.CHIPS * topo.CORES_PER_CHIP)
                if topo.chip(h) == topo.chip(c) and topo.die(h) == topo.die(c) and T.rank_of(h) is None
                and all(topo.may_write(h, d) for d in far)]
        allowed = ~0
        for (d, *_x) in rows + edges:
            if topo.may_write(c, d):
                allowed &= topo.mask(c, d)
        for h in free[:len(far)]:
            allowed &= topo.mask(c, h)
        S = _pick(allowed, K_RANK)
        if not far:
            add(c, [("xa", 16), ("xb", 16)],
                [dict(src=("X", s), dsts=[(d, b, (0, 2))], sem=sem, mask=_m(S[i::2]))
                 for i, (d, s, b, sem, _x) in enumerate(rows)], 1)
            add(c, [("pk", 2)], [dict(src=("EP", full), dsts=[(d, b, full) for (d, b, _u) in edges], sem="se", mask=_m(S))], 2)
            continue
        nfree = 0
        late = []
        for (d, s, b, sem, xs) in rows:
            if topo.may_write(c, d):
                late.append((d, s, b, sem, xs))
                continue
            h = free[nfree]
            nfree += 1
            add(c, [(xs, 16)], [dict(src=("X", s), dsts=[(h, b, (0, 2))], sem=sem, mask=_m(S))], 1)
            relay_jobs.append((h, d, b, (0, 2), sem, sem, 4))
        dsts = []
        for (d, b, u) in edges:
            if not topo.may_write(c, d):
                h = free[nfree]
                nfree += 1
                dsts.insert(0, (h, b, full))
                relay_jobs.append((h, d, b, u, "se", "sel", 5))
            else:
                dsts.append((d, b, full))
        add(c, [("pk", 2)], [dict(src=("EP", full), dsts=dsts, sem="se", mask=_m(S))], 2)
        for (d, s, b, sem, xs) in late:
            add(c, [(xs, 16)], [dict(src=("X", s), dsts=[(d, b, (0, 2))], sem=sem, mask=_m(S))], 3)
    for (h, d, b, u, sin, sout, k) in relay_jobs:
        add(h, [(sin, inc[(h, sin)])],
            [dict(src=(b, u), dsts=[(d, b, u)], sem=sout, mask=_m(_pick(topo.mask(h, d), K_RELAY)))], k)
    return calls, inc, key


def _issue(g, core, T, topo, calls, inc):
    for (waits, transfers) in calls.get(core, []):
        for (s, n) in waits:
            g.wait_ge(T.sem[s], n)
        ts = []
        for t in transfers:
            b, (lo, hi) = t["src"]
            ids, outs = [], []
            for (d, db, (dlo, dhi)) in t["dsts"]:
                rid, pid, _se = topo.addr(d)
                ids.append(DstId(rid=rid, pnc=pid))
                outs.append(T[db][:, dlo:dhi, :])
            ts.append(RemoteDMATransfer(dst_ids=ids, dma_engine_mask=t["mask"], remote_sem=T.sem[t["sem"]],
                                        srcs=[T[b][:, lo:hi, :]], dsts=outs))
        g.remote_dma_fused(ts, local_sem=T.sem.sent)
    if (core, "sent") in inc:
        g.wait_ge(T.sem.sent, inc[(core, "sent")])


def rank_program(g, core, T, topo):
    calls, inc, key = _plan(T, topo)
    rank = T.rank_of(core)
    if rank is None:
        _issue(g, core, T, topo, calls, inc)
        return
    sem = T.sem

    first = calls[core][0][0][0][0]
    for s in ([first] + [q for q in ("xa", "xb") if q != first]):
        h = 0 if s == "xa" else 1
        g.sync.dma_start(T.X[:, 2 * h:2 * h + 2, :], T.x[:, 128 * h:128 * h + 128]).then_inc(sem[s], 16)
    g.sync.dma_start(T.W[:], T.w[:]).then_inc(sem.wl, 16)

    v = g.vector
    v.wait_ge(sem.xa, 16)
    v.wait_ge(sem.xb, 16)
    v.tensor_copy(T.EP[:, :, 0:2], T.X[:, :, WW - 2:WW]).then_inc(sem.pk, 1)
    v.tensor_copy(T.EP[:, :, 2:4], T.X[:, :, 0:2]).then_inc(sem.pk, 1)

    P = (T.P0, T.P1)

    def wt(a, b):
        t = 3 * a + b
        return T.W[:, 128 * t:128 * t + 128]

    def big(h, a, buf, r0):
        return [(h, P[h][:, 0:2, :], wt(a, 1), buf[:, r0:r0 + 2, :]),
                (h, P[h][:, 0:2, 2:WW], wt(a, 0), buf[:, r0:r0 + 2, 0:WW - 2]),
                (h, P[h][:, 0:2, 0:WW - 2], wt(a, 2), buf[:, r0:r0 + 2, 2:WW])]

    def small(h, a, buf, r0):
        return [(h, P[h][:, 0:2, 0:2], wt(a, 0), buf[:, r0:r0 + 2, 0:2]),
                (h, P[h][:, 0:2, WW - 2:WW], wt(a, 2), buf[:, r0:r0 + 2, 2:4])]

    relayed = (core, "sel") in inc
    R, C = divmod(rank, GC)
    eu_far = not topo.may_write(T.cores[_rank(R - 1, C + 1)], core)
    ed_far = not topo.may_write(T.cores[_rank(R + 1, C + 1)], core)
    near = small(0, 1, T.EH, 0) + small(0, 2, T.EH, 2) + small(1, 0, T.EH, 0) + small(1, 1, T.EH, 2)
    farm = []
    (farm if eu_far else near).extend(small(0, 0, T.EU, 2))
    (farm if ed_far else near).extend(small(1, 2, T.ED, 0))
    events = [(key[(core, "su")], "su", big(0, 0, T.U, 0)),
              (key[(core, "sd")], "sd", big(1, 2, T.D, 0)),
              (key[(core, "se")], "se", near)]
    if relayed:
        events.append((key[(core, "sel")], "sel", farm))
    events.sort(key=lambda e: e[0])
    own = big(0, 1, T.X, 0) + big(0, 2, T.X, 2) + big(1, 1, T.X, 2) + big(1, 0, T.X, 0)
    seq = [(None, m) for m in own]
    for (_k, s, ms) in events:
        seq += [(s if i == 0 else None, m) for i, m in enumerate(ms)]
    last = {}
    for i, (_s, m) in enumerate(seq):
        last[m[0]] = i
    te = g.tensor
    te.wait_ge(sem.xa, 16)
    te.wait_ge(sem.xb, 16)
    te.wait_ge(sem.wl, 16)
    opened = set()
    for i, (s, (h, out, lhsT, rhs)) in enumerate(seq):
        if s is not None:
            te.wait_ge(sem[s], inc[(core, s)])
        ins = te.matmul(out, lhsT, rhs, h not in opened, last[h] == i)
        opened.add(h)
        if last[h] == i:
            ins.then_inc(sem["mm%d" % h], 1)

    order = sorted((0, 1), key=lambda h: last[h])
    for h, q in zip(order, (g.scalar, g.sync)):
        Y = T["Y%d" % h]
        v.wait_ge(sem["mm%d" % h], 1)
        v.tensor_copy(Y[:], P[h][:, 0:2, :]).then_inc(sem["ev%d" % h], 1)
        q.wait_ge(sem["ev%d" % h], 1)
        q.dma_start(T.y[:, 128 * h:128 * h + 128], Y[:]).then_inc(sem["st%d" % h], 16)
        q.wait_ge(sem["st%d" % h], 16)

    _issue(g, core, T, topo, calls, inc)
